import numpy as np
import ml_dtypes


def mxq(x, axis, fmt="e4m3"):
    dtype, down = {"e4m3": (ml_dtypes.float8_e4m3fn, 7), "e5m2": (ml_dtypes.float8_e5m2, 14)}[fmt]
    v = np.moveaxis(np.asarray(x, np.float32).astype(ml_dtypes.bfloat16).astype(np.float64), axis, -1)
    blocks = v.reshape(v.shape[:-1] + (-1, 32))
    amax = np.abs(blocks).max(-1, keepdims=True)
    byte = np.maximum(np.where(amax > 0, np.frexp(amax)[1] - 1 + 127, 0) - down, 1)
    scale = np.exp2(byte - 127.0)
    codes = (blocks / scale).astype(np.float32).astype(dtype).astype(np.float64)
    return np.moveaxis((codes * scale).reshape(v.shape), -1, axis)


WIDE = False


def mx_kscale(k):
    if not WIDE:
        return np.ones(k)
    levels = np.array([30, -30])
    if k % 512:
        return np.exp2(np.random.permutation(np.resize(levels, k // 32))).repeat(32)
    a = np.empty((k // 512, 16))
    for p in range(k // 512):
        a[p, :8] = np.random.permutation(np.resize(levels, 8))
        for g in range(8):
            far = levels[np.abs(levels - a[p, g]) >= 10]
            a[p, g + 8] = far[np.random.randint(len(far))]
    return np.exp2(a.ravel()).repeat(32)


def f64(x):
    return np.asarray(x).astype(np.float64)


def striped(idx):
    return np.tile(np.asarray(idx).reshape(-1, 16).T, (8, 1)).astype(np.uint16)


def unstriped(offs):
    return offs[:16].T.reshape(-1).astype(np.int64)


E2M1 = np.array([0.0, 0.5, 1.0, 1.5, 2.0, 3.0, 4.0, 6.0, -0.0, -0.5, -1.0, -1.5, -2.0, -3.0, -4.0, -6.0])


def pack_weight(w, fmt):
    k, n = w.shape
    w = f64(np.asarray(w, np.float32).astype(ml_dtypes.bfloat16)).reshape(k // 32, 32, n)
    amax = np.abs(w).max(1)
    if fmt == "e4m3":
        byte = np.frexp(amax)[1] - 1 + 127 - 7
    else:
        mant, ex = np.frexp(amax / 6.0)
        byte = np.where(mant > 0.5, ex, ex - 1) + 127
    byte = np.clip(np.where(amax > 0, byte, 1), 1, 254)
    scaled = (w * np.exp2(127.0 - byte)[:, None, :]).reshape(k, n).astype(np.float32)
    by_word = np.ascontiguousarray(scaled.reshape(k // 512, 128, 4, n).transpose(0, 1, 3, 2))
    if fmt == "e4m3":
        words = by_word.astype(ml_dtypes.float8_e4m3fn).view(np.uint8)
    else:
        c = by_word.astype(ml_dtypes.float4_e2m1fn).view(np.uint8) & 0xF
        words = (c[..., 0::2] | (c[..., 1::2] << 4)).reshape(k // 512, 128, 2 * n)
    return np.ascontiguousarray(words), np.ascontiguousarray(byte.astype(np.uint8).reshape(k // 512, 16, n))


def unpack_weight(words, scales, fmt):
    g, _, n = scales.shape
    words = np.ascontiguousarray(words).reshape(g, 128, n, -1)
    if fmt == "e4m3":
        vals = words.view(ml_dtypes.float8_e4m3fn).astype(np.float64)
    else:
        nib = np.empty((g, 128, n, 4), np.uint8)
        nib[..., 0::2] = words & 0xF
        nib[..., 1::2] = words >> 4
        vals = E2M1[nib]
    vals = vals * np.repeat(np.exp2(scales.astype(np.float64) - 127.0), 8, axis=1)[..., None]
    return vals.transpose(0, 1, 3, 2).reshape(g * 512, n)


K, T, J, S, R, V, N = 1024, 1024, 256, 512, 512, 512, 256


def setup_inputs():
    n = np.random.standard_normal
    idx = np.random.permutation(T)[:J]
    idx2 = np.random.permutation(S)[:J]
    idx3 = np.random.permutation(V)[:J]
    fk = mx_kscale(K)
    fr = mx_kscale(R)
    wp = pack_weight(n((K, R)) * 1 / np.sqrt(K) * fk[:, None] * fr, "e2m1")
    wbp = pack_weight(n((R, N)) * 1 / np.sqrt(R) / fr[:, None], "e4m3")
    return {
        "xa": (n((K, T))).astype(np.float32),
        "xb": (n((K, S))).astype(np.float32),
        "fk": (np.random.uniform(0.5, 2.0, (K, 1)) / fk[:, None]).astype(np.float32),
        "w_words": wp[0],
        "w_scales": wp[1],
        "tb": (n((R, V)) * 0.7 * fr[:, None]).astype(np.float32),
        "wb_words": wbp[0],
        "wb_scales": wbp[1],
        "rs": (1.0 * n((J, N))).astype(np.float32),
        "offs": striped(idx),
        "offs2": striped(idx2),
        "offs3": striped(idx3),
    }


def reference(xa, xb, fk, w_words, w_scales, tb, wb_words, wb_scales, rs, offs, offs2, offs3):
    idx = unstriped(offs)
    idx2 = unstriped(offs2)
    idx3 = unstriped(offs3)
    wu = unpack_weight(w_words, w_scales, "e2m1")
    wbu = unpack_weight(wb_words, wb_scales, "e4m3")
    u = f64(xa)[:, idx] * f64(xb)[:, idx2] * f64(fk)
    uq = mxq(u, 0, "e4m3")
    a = wu.T @ uq
    hid = np.maximum(a, f64(tb)[:, idx3])
    hidq = mxq(hid, 0, "e5m2")
    p = hidq.T @ wbu
    pk2 = np.max(np.abs(p), axis=1, keepdims=True)
    y = p / (pk2 + 0.2) + 0.3 * f64(rs)
    return y

@@ -1,0 +1,169 @@
+from contextlib import ExitStack
+
+import concourse.mybir as mybir
+
+K, T, J, S, R, V, N = 1024, 1024, 256, 512, 512, 512, 256
+FLOPS = 2 * K * R * J + 2 * R * J * N
+
+F32 = mybir.dt.float32
+BF16 = mybir.dt.bfloat16
+I32 = mybir.dt.int32
+U32 = mybir.dt.uint32
+U16 = mybir.dt.uint16
+U8 = mybir.dt.uint8
+E4M3 = mybir.dt.float8_e4m3fn_x4
+E5M2 = mybir.dt.float8_e5m2_x4
+E2M1 = mybir.dt.float4_e2m1fn_x4
+ALU = mybir.AluOpType
+ACT = mybir.ActivationFunctionType
+
+P = 128
+PACK = 4
+PASSES = K // (P * PACK)
+HALVES = J // P
+LIST_COLS = J // 16
+RUN = 4
+
+
+def tile_list_entryproducts_abovetable_rowpeaks_kernel(
+    tc, xa, xb, fk, w_words, w_scales, tb, wb_words, wb_scales, rs, offs, offs2, offs3, out
+):
+    nc = tc.nc
+    with ExitStack() as ctx:
+        sb = ctx.enter_context(tc.tile_pool(name="sb", bufs=1))
+        ps = ctx.enter_context(tc.psum_pool(name="ps", bufs=1))
+
+        def half_cols(h):
+            return slice(h * P, (h + 1) * P)
+
+        def half_list(lst, h):
+            return lst[:, h * LIST_COLS // HALVES : (h + 1) * LIST_COLS // HALVES]
+
+        def woven(t):
+            return t.rearrange("p (c i t) -> p c t i", i=RUN, t=PACK)
+
+        def planes(t):
+            return t.rearrange("p t (c i) -> p c t i", i=RUN)
+
+        list_a = sb.tile([P, LIST_COLS], U16, name="list_a")
+        list_b = sb.tile([P, LIST_COLS], U16, name="list_b")
+        list_t = sb.tile([P, LIST_COLS], U16, name="list_t")
+
+        xa_rows = xa.rearrange("(a p t) c -> a t p c", p=P, t=PACK)
+        xb_rows = xb.rearrange("(a p t) c -> a p t c", p=P, t=PACK)
+        tb_rows = tb.rearrange("(p t) c -> t p c", t=PACK)
+
+        xa_sb = [[sb.tile([P, T], F32, name=f"xa{a}{t}") for t in range(PACK)] for a in range(PASSES)]
+        xb_sb = [sb.tile([P, PACK, S], F32, name=f"xb{a}") for a in range(PASSES)]
+        tb_sb = [sb.tile([P, V], F32, name=f"tb{t}") for t in range(PACK)]
+        w_raw = sb.tile([P, PASSES, 2 * R], U8, name="w_raw")
+        ws_raw = sb.tile([P, PASSES, R], U8, name="ws_raw")
+        wb_codes = sb.tile([P, N], U32, name="wb_codes", align_bytes=64)
+        wb_sc = sb.tile([P, N], U8, name="wb_sc", align_bytes=64)
+        fk_sb = sb.tile([P, PASSES, PACK], F32, name="fk_sb")
+        rs_sb = sb.tile([P, HALVES, N], F32, name="rs_sb")
+
+        nc.gpsimd.dma_start(out=fk_sb[:], in_=fk.rearrange("(a p t) o -> p a (t o)", p=P, t=PACK))
+        nc.gpsimd.memset(ws_raw[:].bitcast(I32), 0)
+        nc.gpsimd.memset(wb_sc[:].bitcast(I32), 0)
+        ws_rows = w_scales.bitcast(I32).rearrange("a q c -> q a c")
+        wbs_rows = wb_scales[0].bitcast(I32)
+        for q in range(4):
+            nc.gpsimd.dma_start(out=ws_raw[32 * q : 32 * q + 4].bitcast(I32), in_=ws_rows[4 * q : 4 * q + 4])
+        for q in range(4):
+            nc.gpsimd.dma_start(out=wb_sc[32 * q : 32 * q + 4, :].bitcast(I32), in_=wbs_rows[4 * q : 4 * q + 4])
+
+        nc.sync.dma_start(out=xb_sb[0][:], in_=xb_rows[0])
+        nc.sync.dma_start(list_b[:], offs2)
+        nc.sync.dma_start(list_a[:], offs)
+        nc.sync.dma_start(list_t[:], offs3)
+        nc.sync.dma_start(out=w_raw[:].bitcast(I32), in_=w_words.bitcast(I32).rearrange("a p c -> p a c"))
+        nc.sync.dma_start(out=xb_sb[1][:], in_=xb_rows[1])
+        for a in range(PASSES):
+            for t in range(PACK):
+                nc.sync.dma_start(out=xa_sb[a][t][:], in_=xa_rows[a, t])
+        for t in range(PACK):
+            nc.sync.dma_start(out=tb_sb[t][:], in_=tb_rows[t])
+        nc.sync.dma_start(out=wb_codes[:].bitcast(I32), in_=wb_words[0].rearrange("p n t -> p (n t)").bitcast(I32))
+        nc.sync.dma_start(out=rs_sb[:], in_=rs.rearrange("(h p) n -> p h n", p=P))
+
+        w_codes = sb.tile([P, PASSES, PACK, 2 * P], U8, name="w_codes", align_bytes=64)
+        w_sc = sb.tile([P, PASSES, PACK, P], U8, name="w_sc", align_bytes=64)
+        for a in range(PASSES):
+            nc.vector.tensor_copy(
+                out=w_codes[:, a].rearrange("p t (m e) -> p t m e", e=2),
+                in_=w_raw[:, a, :].rearrange("p (m t e) -> p t m e", t=PACK, e=2),
+            )
+        nc.vector.tensor_copy(out=w_sc[:], in_=ws_raw[:].rearrange("p a (m t) -> p a t m", t=PACK))
+
+        bf = [[None] * PACK for a in range(PASSES)]
+        for a in range(PASSES):
+            for t in range(PACK):
+                picked = sb.tile([P, J], F32, name=f"picked{a}{t}")
+                nc.scalar.activation(picked[:], xb_sb[a][:, t, :].indirect(list_b[:]), ACT.Copy)
+                bf[a][t] = sb.tile([P, J], F32, name=f"bf{a}{t}")
+                nc.scalar.activation(bf[a][t][:], picked[:], ACT.Copy, scale=fk_sb[:, a, t : t + 1])
+
+        acc = [ps.tile([P, PACK, P], F32, name=f"acc{h}") for h in range(HALVES)]
+        for a in range(PASSES):
+            u = [sb.tile([P, PACK, P], F32, name=f"u{a}{h}") for h in range(HALVES)]
+            for t in range(PACK):
+                for h in range(HALVES):
+                    nc.vector.tensor_tensor(
+                        u[h][:, t, :], xa_sb[a][t][:].indirect(half_list(list_a, h)), bf[a][t][:, half_cols(h)], ALU.mult
+                    )
+            u_bf = [sb.tile([P, PACK * P], BF16, name=f"u_bf{a}{h}", align_bytes=64) for h in range(HALVES)]
+            for h in range(HALVES):
+                nc.vector.tensor_copy(out=woven(u_bf[h][:]), in_=planes(u[h][:]))
+            for h in range(HALVES):
+                u_codes = sb.tile([P, P], U32, name=f"u_codes{a}{h}", align_bytes=64)
+                u_sc = sb.tile([P, P], U8, name=f"u_sc{a}{h}", align_bytes=64)
+                nc.vector.quantize_mx(out=u_codes[:].bitcast(E4M3), scales=u_sc[:], in_=u_bf[h][:])
+                for t in range(PACK):
+                    nc.tensor.matmul_mx(
+                        out=acc[h][:, t, :],
+                        lhsT=w_codes[:, a, t, :].bitcast(E2M1),
+                        lhsT_scale=w_sc[:, a, t, :],
+                        rhs=u_codes[:].bitcast(E4M3),
+                        rhs_scale=u_sc[:],
+                        start=(a == 0 and t == 0),
+                        stop=(a == PASSES - 1 and t == PACK - 1),
+                    )
+
+        floor = [sb.tile([P, PACK, P], F32, name=f"floor{h}") for h in range(HALVES)]
+        for t in range(PACK):
+            for h in range(HALVES):
+                nc.scalar.activation(floor[h][:, t, :], tb_sb[t][:].indirect(half_list(list_t, h)), ACT.Copy)
+
+        resid = [sb.tile([P, N], F32, name=f"resid{h}") for h in range(HALVES)]
+        for h in range(HALVES):
+            nc.scalar.activation(resid[h][:], rs_sb[:, h, :], ACT.Copy, scale=0.3)
+
+        hid = [sb.tile([P, PACK * P], BF16, name=f"hid{h}", align_bytes=64) for h in range(HALVES)]
+        for h in range(HALVES):
+            nc.vector.tensor_tensor(woven(hid[h][:]), planes(acc[h][:]), planes(floor[h][:]), ALU.max)
+        prod = [ps.tile([P, N], F32, name=f"prod{h}") for h in range(HALVES)]
+        for h in range(HALVES):
+            hid_codes = sb.tile([P, P], U32, name=f"hid_codes{h}", align_bytes=64)
+            hid_sc = sb.tile([P, P], U8, name=f"hid_sc{h}", align_bytes=64)
+            nc.vector.quantize_mx(out=hid_codes[:].bitcast(E5M2), scales=hid_sc[:], in_=hid[h][:])
+            nc.tensor.matmul_mx(
+                out=prod[h][:],
+                lhsT=hid_codes[:].bitcast(E5M2),
+                lhsT_scale=hid_sc[:],
+                rhs=wb_codes[:].bitcast(E4M3),
+                rhs_scale=wb_sc[:],
+                start=True,
+                stop=True,
+            )
+        for h in range(HALVES):
+            size = sb.tile([P, N], F32, name=f"size{h}")
+            nc.scalar.activation(size[:], prod[h][:], ACT.Abs)
+            shifted = sb.tile([P, N], F32, name=f"shifted{h}")
+            denom = sb.tile([P, 1], F32, name=f"denom{h}")
+            nc.vector.tensor_scalar(shifted[:], size[:], 0.2, None, ALU.add, ALU.max, accum_out=denom[:])
+            inv = sb.tile([P, 1], F32, name=f"inv{h}")
+            nc.vector.reciprocal(inv[:], denom[:])
+            y = sb.tile([P, N], F32, name=f"y{h}")
+            nc.vector.scalar_tensor_tensor(y[:], prod[h][:], inv[:], resid[h][:], ALU.mult, ALU.add)
+            nc.sync.dma_start(out=out[half_cols(h), :], in_=y[:])

@@ -63,25 +63,24 @@ def tile_list_entryproducts_abovetable_rowpeaks_kernel(
         fk_sb = sb.tile([P, PASSES, PACK], F32, name="fk_sb")
         rs_sb = sb.tile([P, HALVES, N], F32, name="rs_sb")
 
-        nc.gpsimd.dma_start(out=fk_sb[:], in_=fk.rearrange("(a p t) o -> p a (t o)", p=P, t=PACK))
         nc.gpsimd.memset(ws_raw[:].bitcast(I32), 0)
         nc.gpsimd.memset(wb_sc[:].bitcast(I32), 0)
         ws_rows = w_scales.bitcast(I32).rearrange("a q c -> q a c")
         wbs_rows = wb_scales[0].bitcast(I32)
-        for q in range(4):
-            nc.gpsimd.dma_start(out=ws_raw[32 * q : 32 * q + 4].bitcast(I32), in_=ws_rows[4 * q : 4 * q + 4])
-        for q in range(4):
-            nc.gpsimd.dma_start(out=wb_sc[32 * q : 32 * q + 4, :].bitcast(I32), in_=wbs_rows[4 * q : 4 * q + 4])
 
         nc.sync.dma_start(out=xb_sb[0][:], in_=xb_rows[0])
         nc.sync.dma_start(list_b[:], offs2)
-        nc.sync.dma_start(list_a[:], offs)
-        nc.sync.dma_start(list_t[:], offs3)
+        nc.sync.dma_start(out=fk_sb[:], in_=fk.rearrange("(a p t) o -> p a (t o)", p=P, t=PACK))
         nc.sync.dma_start(out=w_raw[:].bitcast(I32), in_=w_words.bitcast(I32).rearrange("a p c -> p a c"))
         nc.sync.dma_start(out=xb_sb[1][:], in_=xb_rows[1])
-        for a in range(PASSES):
-            for t in range(PACK):
-                nc.sync.dma_start(out=xa_sb[a][t][:], in_=xa_rows[a, t])
+        nc.sync.dma_start(list_a[:], offs)
+        for q in range(4):
+            nc.sync.dma_start(out=xa_sb[0][q][:], in_=xa_rows[0, q])
+            nc.sync.dma_start(out=ws_raw[32 * q : 32 * q + 4].bitcast(I32), in_=ws_rows[4 * q : 4 * q + 4])
+        nc.sync.dma_start(list_t[:], offs3)
+        for q in range(4):
+            nc.sync.dma_start(out=wb_sc[32 * q : 32 * q + 4, :].bitcast(I32), in_=wbs_rows[4 * q : 4 * q + 4])
+            nc.sync.dma_start(out=xa_sb[1][q][:], in_=xa_rows[1, q])
         for t in range(PACK):
             nc.sync.dma_start(out=tb_sb[t][:], in_=tb_rows[t])
         nc.sync.dma_start(out=wb_codes[:].bitcast(I32), in_=wb_words[0].rearrange("p n t -> p (n t)").bitcast(I32))
@@ -91,10 +90,9 @@ def tile_list_entryproducts_abovetable_rowpeaks_kernel(
         w_sc = sb.tile([P, PASSES, PACK, P], U8, name="w_sc", align_bytes=64)
         for a in range(PASSES):
             nc.vector.tensor_copy(
-                out=w_codes[:, a].rearrange("p t (m e) -> p t m e", e=2),
-                in_=w_raw[:, a, :].rearrange("p (m t e) -> p t m e", t=PACK, e=2),
+                out=w_codes[:, a].bitcast(U16),
+                in_=w_raw[:, a, :].bitcast(U16).rearrange("p (m t) -> p t m", t=PACK),
             )
-        nc.vector.tensor_copy(out=w_sc[:], in_=ws_raw[:].rearrange("p a (m t) -> p a t m", t=PACK))
 
         bf = [[None] * PACK for a in range(PASSES)]
         for a in range(PASSES):
@@ -112,6 +110,7 @@ def tile_list_entryproducts_abovetable_rowpeaks_kernel(
                     nc.vector.tensor_tensor(
                         u[h][:, t, :], xa_sb[a][t][:].indirect(half_list(list_a, h)), bf[a][t][:, half_cols(h)], ALU.mult
                     )
+            nc.vector.tensor_copy(out=w_sc[:, a], in_=ws_raw[:, a, :].rearrange("p (m t) -> p t m", t=PACK))
             u_bf = [sb.tile([P, PACK * P], BF16, name=f"u_bf{a}{h}", align_bytes=64) for h in range(HALVES)]
             for h in range(HALVES):
                 nc.vector.tensor_copy(out=woven(u_bf[h][:]), in_=planes(u[h][:]))

@@ -23,6 +23,7 @@ PASSES = K // (P * PACK)
 HALVES = J // P
 LIST_COLS = J // 16
 RUN = 4
+XA_LOADS = [(0, 0, 2), (0, 2, 2), (1, 0, 1), (1, 1, 1), (1, 2, 1), (1, 3, 1)]
 
 
 def tile_list_entryproducts_abovetable_rowpeaks_kernel(
@@ -49,38 +50,39 @@ def tile_list_entryproducts_abovetable_rowpeaks_kernel(
         list_b = sb.tile([P, LIST_COLS], U16, name="list_b")
         list_t = sb.tile([P, LIST_COLS], U16, name="list_t")
 
-        xa_rows = xa.rearrange("(a p t) c -> a t p c", p=P, t=PACK)
+        xa_rows = xa.rearrange("(a p t) c -> a p (t c)", p=P, t=PACK)
         xb_rows = xb.rearrange("(a p t) c -> a p t c", p=P, t=PACK)
         tb_rows = tb.rearrange("(p t) c -> t p c", t=PACK)
 
-        xa_sb = [[sb.tile([P, T], F32, name=f"xa{a}{t}") for t in range(PACK)] for a in range(PASSES)]
+        xa_sb = [sb.tile([P, n * T], F32, name=f"xa{a}{t}") for a, t, n in XA_LOADS]
         xb_sb = [sb.tile([P, PACK, S], F32, name=f"xb{a}") for a in range(PASSES)]
         tb_sb = [sb.tile([P, V], F32, name=f"tb{t}") for t in range(PACK)]
         w_raw = sb.tile([P, PASSES, 2 * R], U8, name="w_raw")
         ws_raw = sb.tile([P, PASSES, R], U8, name="ws_raw")
         wb_codes = sb.tile([P, N], U32, name="wb_codes", align_bytes=64)
         wb_sc = sb.tile([P, N], U8, name="wb_sc", align_bytes=64)
-        fk_sb = sb.tile([P, PASSES, PACK], F32, name="fk_sb")
+        fk_sb = sb.tile([P, PASSES, 2 * PACK], F32, name="fk_sb")
         rs_sb = sb.tile([P, HALVES, N], F32, name="rs_sb")
 
         nc.gpsimd.memset(ws_raw[:].bitcast(I32), 0)
         nc.gpsimd.memset(wb_sc[:].bitcast(I32), 0)
-        ws_rows = w_scales.bitcast(I32).rearrange("a q c -> q a c")
-        wbs_rows = wb_scales[0].bitcast(I32)
+        ws_rows = w_scales.bitcast(I32).rearrange("a (q r) c -> r q a c", r=4)
+        wbs_rows = wb_scales[0].bitcast(I32).rearrange("(q r) c -> r q c", r=4)
+        nc.scalar.dma_start(out=fk_sb[:, :, 0:PACK], in_=fk.rearrange("(a p t) o -> p a (t o)", p=P, t=PACK))
+        for r in range(4):
+            nc.gpsimd.dma_start(out=ws_raw[r:P:32].bitcast(I32), in_=ws_rows[r])
+        for r in range(4):
+            nc.gpsimd.dma_start(out=wb_sc[r:P:32, :].bitcast(I32), in_=wbs_rows[r])
 
         nc.sync.dma_start(out=xb_sb[0][:], in_=xb_rows[0])
         nc.sync.dma_start(list_b[:], offs2)
-        nc.sync.dma_start(out=fk_sb[:], in_=fk.rearrange("(a p t) o -> p a (t o)", p=P, t=PACK))
         nc.sync.dma_start(out=w_raw[:].bitcast(I32), in_=w_words.bitcast(I32).rearrange("a p c -> p a c"))
-        nc.sync.dma_start(out=xb_sb[1][:], in_=xb_rows[1])
         nc.sync.dma_start(list_a[:], offs)
-        for q in range(4):
-            nc.sync.dma_start(out=xa_sb[0][q][:], in_=xa_rows[0, q])
-            nc.sync.dma_start(out=ws_raw[32 * q : 32 * q + 4].bitcast(I32), in_=ws_rows[4 * q : 4 * q + 4])
-        nc.sync.dma_start(list_t[:], offs3)
-        for q in range(4):
-            nc.sync.dma_start(out=wb_sc[32 * q : 32 * q + 4, :].bitcast(I32), in_=wbs_rows[4 * q : 4 * q + 4])
-            nc.sync.dma_start(out=xa_sb[1][q][:], in_=xa_rows[1, q])
+        for g, (a, t, n) in enumerate(XA_LOADS):
+            if g == 2:
+                nc.sync.dma_start(out=xb_sb[1][:], in_=xb_rows[1])
+                nc.sync.dma_start(list_t[:], offs3)
+            nc.sync.dma_start(out=xa_sb[g][:], in_=xa_rows[a][:, t * T : (t + n) * T])
         for t in range(PACK):
             nc.sync.dma_start(out=tb_sb[t][:], in_=tb_rows[t])
         nc.sync.dma_start(out=wb_codes[:].bitcast(I32), in_=wb_words[0].rearrange("p n t -> p (n t)").bitcast(I32))
@@ -103,17 +105,34 @@ def tile_list_entryproducts_abovetable_rowpeaks_kernel(
                 nc.scalar.activation(bf[a][t][:], picked[:], ACT.Copy, scale=fk_sb[:, a, t : t + 1])
 
         acc = [ps.tile([P, PACK, P], F32, name=f"acc{h}") for h in range(HALVES)]
-        for a in range(PASSES):
-            u = [sb.tile([P, PACK, P], F32, name=f"u{a}{h}") for h in range(HALVES)]
-            for t in range(PACK):
+        u = [sb.tile([P, PACK, J], F32, name=f"u{a}") for a in range(PASSES)]
+
+        def products(g):
+            a, t, n = XA_LOADS[g]
+            if g == len(XA_LOADS) - 1:
                 for h in range(HALVES):
                     nc.vector.tensor_tensor(
-                        u[h][:, t, :], xa_sb[a][t][:].indirect(half_list(list_a, h)), bf[a][t][:, half_cols(h)], ALU.mult
+                        u[a][:, t, half_cols(h)],
+                        xa_sb[g][:].indirect(half_list(list_a, h)),
+                        bf[a][t][:, half_cols(h)],
+                        ALU.mult,
                     )
+            else:
+                nc.vector.tensor_tensor(u[a][:, t, :], xa_sb[g][:].indirect(list_a[:]), bf[a][t][:], ALU.mult)
+            if n == 2:
+                second = sb.tile([P, J], F32, name=f"second{g}")
+                nc.vector.tensor_copy(second[:], xa_sb[g][:, T : 2 * T].indirect(list_a[:]))
+                nc.vector.tensor_tensor(u[a][:, t + 1, :], second[:], bf[a][t + 1][:], ALU.mult)
+
+        for a in range(PASSES):
             nc.vector.tensor_copy(out=w_sc[:, a], in_=ws_raw[:, a, :].rearrange("p (m t) -> p t m", t=PACK))
+        for a in range(PASSES):
+            for g in range(len(XA_LOADS)):
+                if XA_LOADS[g][0] == a:
+                    products(g)
             u_bf = [sb.tile([P, PACK * P], BF16, name=f"u_bf{a}{h}", align_bytes=64) for h in range(HALVES)]
             for h in range(HALVES):
-                nc.vector.tensor_copy(out=woven(u_bf[h][:]), in_=planes(u[h][:]))
+                nc.vector.tensor_copy(out=woven(u_bf[h][:]), in_=planes(u[a][:, :, half_cols(h)]))
             for h in range(HALVES):
                 u_codes = sb.tile([P, P], U32, name=f"u_codes{a}{h}", align_bytes=64)
                 u_sc = sb.tile([P, P], U8, name=f"u_sc{a}{h}", align_bytes=64)
@@ -129,10 +148,13 @@ def tile_list_entryproducts_abovetable_rowpeaks_kernel(
                         stop=(a == PASSES - 1 and t == PACK - 1),
                     )
 
-        floor = [sb.tile([P, PACK, P], F32, name=f"floor{h}") for h in range(HALVES)]
-        for t in range(PACK):
-            for h in range(HALVES):
-                nc.scalar.activation(floor[h][:, t, :], tb_sb[t][:].indirect(half_list(list_t, h)), ACT.Copy)
+        floor = sb.tile([P, PACK, J], F32, name="floor")
+        for t in range(PACK - 1):
+            nc.scalar.activation(floor[:, t, :], tb_sb[t][:].indirect(list_t[:]), ACT.Copy)
+        for h in range(HALVES):
+            nc.scalar.activation(
+                floor[:, PACK - 1, half_cols(h)], tb_sb[PACK - 1][:].indirect(half_list(list_t, h)), ACT.Copy
+            )
 
         resid = [sb.tile([P, N], F32, name=f"resid{h}") for h in range(HALVES)]
         for h in range(HALVES):
@@ -140,7 +162,7 @@ def tile_list_entryproducts_abovetable_rowpeaks_kernel(
 
         hid = [sb.tile([P, PACK * P], BF16, name=f"hid{h}", align_bytes=64) for h in range(HALVES)]
         for h in range(HALVES):
-            nc.vector.tensor_tensor(woven(hid[h][:]), planes(acc[h][:]), planes(floor[h][:]), ALU.max)
+            nc.vector.tensor_tensor(woven(hid[h][:]), planes(acc[h][:]), planes(floor[:, :, half_cols(h)]), ALU.max)
         prod = [ps.tile([P, N], F32, name=f"prod{h}") for h in range(HALVES)]
         for h in range(HALVES):
             hid_codes = sb.tile([P, P], U32, name=f"hid_codes{h}", align_bytes=64)

from contextlib import ExitStack

import concourse.mybir as mybir

K, T, J, S, R, V, N = 1024, 1024, 256, 512, 512, 512, 256
FLOPS = 2 * K * R * J + 2 * R * J * N

F32 = mybir.dt.float32
BF16 = mybir.dt.bfloat16
I32 = mybir.dt.int32
U32 = mybir.dt.uint32
U16 = mybir.dt.uint16
U8 = mybir.dt.uint8
E4M3 = mybir.dt.float8_e4m3fn_x4
E5M2 = mybir.dt.float8_e5m2_x4
E2M1 = mybir.dt.float4_e2m1fn_x4
ALU = mybir.AluOpType
ACT = mybir.ActivationFunctionType

P = 128
PACK = 4
PASSES = K // (P * PACK)
HALVES = J // P
LIST_COLS = J // 16
RUN = 4
XA_LOADS = [(0, 0, 2), (0, 2, 2), (1, 0, 1), (1, 1, 1), (1, 2, 1), (1, 3, 1)]


def tile_list_entryproducts_abovetable_rowpeaks_kernel(
    tc, xa, xb, fk, w_words, w_scales, tb, wb_words, wb_scales, rs, offs, offs2, offs3, out
):
    nc = tc.nc
    with ExitStack() as ctx:
        sb = ctx.enter_context(tc.tile_pool(name="sb", bufs=1))
        ps = ctx.enter_context(tc.psum_pool(name="ps", bufs=1))

        def half_cols(h):
            return slice(h * P, (h + 1) * P)

        def half_list(lst, h):
            return lst[:, h * LIST_COLS // HALVES : (h + 1) * LIST_COLS // HALVES]

        def woven(t):
            return t.rearrange("p (c i t) -> p c t i", i=RUN, t=PACK)

        def planes(t):
            return t.rearrange("p t (c i) -> p c t i", i=RUN)

        list_a = sb.tile([P, LIST_COLS], U16, name="list_a")
        list_b = sb.tile([P, LIST_COLS], U16, name="list_b")
        list_t = sb.tile([P, LIST_COLS], U16, name="list_t")

        xa_rows = xa.rearrange("(a p t) c -> a p (t c)", p=P, t=PACK)
        xb_rows = xb.rearrange("(a p t) c -> a p t c", p=P, t=PACK)
        tb_rows = tb.rearrange("(p t) c -> t p c", t=PACK)

        xa_sb = [sb.tile([P, n * T], F32, name=f"xa{a}{t}") for a, t, n in XA_LOADS]
        xb_sb = [sb.tile([P, PACK, S], F32, name=f"xb{a}") for a in range(PASSES)]
        tb_sb = [sb.tile([P, V], F32, name=f"tb{t}") for t in range(PACK)]
        w_raw = sb.tile([P, PASSES, 2 * R], U8, name="w_raw")
        ws_raw = sb.tile([P, PASSES, R], U8, name="ws_raw")
        wb_codes = sb.tile([P, N], U32, name="wb_codes", align_bytes=64)
        wb_sc = sb.tile([P, N], U8, name="wb_sc", align_bytes=64)
        fk_sb = sb.tile([P, PASSES, 2 * PACK], F32, name="fk_sb")
        rs_sb = sb.tile([P, HALVES, N], F32, name="rs_sb")

        nc.gpsimd.memset(ws_raw[:].bitcast(I32), 0)
        nc.gpsimd.memset(wb_sc[:].bitcast(I32), 0)
        ws_rows = w_scales.bitcast(I32).rearrange("a (q r) c -> r q a c", r=4)
        wbs_rows = wb_scales[0].bitcast(I32).rearrange("(q r) c -> r q c", r=4)
        nc.scalar.dma_start(out=fk_sb[:, :, 0:PACK], in_=fk.rearrange("(a p t) o -> p a (t o)", p=P, t=PACK))
        for r in range(4):
            nc.gpsimd.dma_start(out=ws_raw[r:P:32].bitcast(I32), in_=ws_rows[r])
        for r in range(4):
            nc.gpsimd.dma_start(out=wb_sc[r:P:32, :].bitcast(I32), in_=wbs_rows[r])

        nc.sync.dma_start(out=xb_sb[0][:], in_=xb_rows[0])
        nc.sync.dma_start(list_b[:], offs2)
        nc.sync.dma_start(out=w_raw[:].bitcast(I32), in_=w_words.bitcast(I32).rearrange("a p c -> p a c"))
        nc.sync.dma_start(list_a[:], offs)
        for g, (a, t, n) in enumerate(XA_LOADS):
            if g == 2:
                nc.sync.dma_start(out=xb_sb[1][:], in_=xb_rows[1])
                nc.sync.dma_start(list_t[:], offs3)
            nc.sync.dma_start(out=xa_sb[g][:], in_=xa_rows[a][:, t * T : (t + n) * T])
        for t in range(PACK):
            nc.sync.dma_start(out=tb_sb[t][:], in_=tb_rows[t])
        nc.sync.dma_start(out=wb_codes[:].bitcast(I32), in_=wb_words[0].rearrange("p n t -> p (n t)").bitcast(I32))
        nc.sync.dma_start(out=rs_sb[:], in_=rs.rearrange("(h p) n -> p h n", p=P))

        w_codes = sb.tile([P, PASSES, PACK, 2 * P], U8, name="w_codes", align_bytes=64)
        w_sc = sb.tile([P, PASSES, PACK, P], U8, name="w_sc", align_bytes=64)
        for a in range(PASSES):
            nc.vector.tensor_copy(
                out=w_codes[:, a].bitcast(U16),
                in_=w_raw[:, a, :].bitcast(U16).rearrange("p (m t) -> p t m", t=PACK),
            )

        bf = [[None] * PACK for a in range(PASSES)]
        for a in range(PASSES):
            for t in range(PACK):
                picked = sb.tile([P, J], F32, name=f"picked{a}{t}")
                nc.scalar.activation(picked[:], xb_sb[a][:, t, :].indirect(list_b[:]), ACT.Copy)
                bf[a][t] = sb.tile([P, J], F32, name=f"bf{a}{t}")
                nc.scalar.activation(bf[a][t][:], picked[:], ACT.Copy, scale=fk_sb[:, a, t : t + 1])

        acc = [ps.tile([P, PACK, P], F32, name=f"acc{h}") for h in range(HALVES)]
        u = [sb.tile([P, PACK, J], F32, name=f"u{a}") for a in range(PASSES)]

        def products(g):
            a, t, n = XA_LOADS[g]
            if g == len(XA_LOADS) - 1:
                for h in range(HALVES):
                    nc.vector.tensor_tensor(
                        u[a][:, t, half_cols(h)],
                        xa_sb[g][:].indirect(half_list(list_a, h)),
                        bf[a][t][:, half_cols(h)],
                        ALU.mult,
                    )
            else:
                nc.vector.tensor_tensor(u[a][:, t, :], xa_sb[g][:].indirect(list_a[:]), bf[a][t][:], ALU.mult)
            if n == 2:
                second = sb.tile([P, J], F32, name=f"second{g}")
                nc.vector.tensor_copy(second[:], xa_sb[g][:, T : 2 * T].indirect(list_a[:]))
                nc.vector.tensor_tensor(u[a][:, t + 1, :], second[:], bf[a][t + 1][:], ALU.mult)

        for a in range(PASSES):
            nc.vector.tensor_copy(out=w_sc[:, a], in_=ws_raw[:, a, :].rearrange("p (m t) -> p t m", t=PACK))
        for a in range(PASSES):
            for g in range(len(XA_LOADS)):
                if XA_LOADS[g][0] == a:
                    products(g)
            u_bf = [sb.tile([P, PACK * P], BF16, name=f"u_bf{a}{h}", align_bytes=64) for h in range(HALVES)]
            for h in range(HALVES):
                nc.vector.tensor_copy(out=woven(u_bf[h][:]), in_=planes(u[a][:, :, half_cols(h)]))
            for h in range(HALVES):
                u_codes = sb.tile([P, P], U32, name=f"u_codes{a}{h}", align_bytes=64)
                u_sc = sb.tile([P, P], U8, name=f"u_sc{a}{h}", align_bytes=64)
                nc.vector.quantize_mx(out=u_codes[:].bitcast(E4M3), scales=u_sc[:], in_=u_bf[h][:])
                for t in range(PACK):
                    nc.tensor.matmul_mx(
                        out=acc[h][:, t, :],
                        lhsT=w_codes[:, a, t, :].bitcast(E2M1),
                        lhsT_scale=w_sc[:, a, t, :],
                        rhs=u_codes[:].bitcast(E4M3),
                        rhs_scale=u_sc[:],
                        start=(a == 0 and t == 0),
                        stop=(a == PASSES - 1 and t == PACK - 1),
                    )

        floor = sb.tile([P, PACK, J], F32, name="floor")
        for t in range(PACK - 1):
            nc.scalar.activation(floor[:, t, :], tb_sb[t][:].indirect(list_t[:]), ACT.Copy)
        for h in range(HALVES):
            nc.scalar.activation(
                floor[:, PACK - 1, half_cols(h)], tb_sb[PACK - 1][:].indirect(half_list(list_t, h)), ACT.Copy
            )

        resid = [sb.tile([P, N], F32, name=f"resid{h}") for h in range(HALVES)]
        for h in range(HALVES):
            nc.scalar.activation(resid[h][:], rs_sb[:, h, :], ACT.Copy, scale=0.3)

        hid = [sb.tile([P, PACK * P], BF16, name=f"hid{h}", align_bytes=64) for h in range(HALVES)]
        for h in range(HALVES):
            nc.vector.tensor_tensor(woven(hid[h][:]), planes(acc[h][:]), planes(floor[:, :, half_cols(h)]), ALU.max)
        prod = [ps.tile([P, N], F32, name=f"prod{h}") for h in range(HALVES)]
        for h in range(HALVES):
            hid_codes = sb.tile([P, P], U32, name=f"hid_codes{h}", align_bytes=64)
            hid_sc = sb.tile([P, P], U8, name=f"hid_sc{h}", align_bytes=64)
            nc.vector.quantize_mx(out=hid_codes[:].bitcast(E5M2), scales=hid_sc[:], in_=hid[h][:])
            nc.tensor.matmul_mx(
                out=prod[h][:],
                lhsT=hid_codes[:].bitcast(E5M2),
                lhsT_scale=hid_sc[:],
                rhs=wb_codes[:].bitcast(E4M3),
                rhs_scale=wb_sc[:],
                start=True,
                stop=True,
            )
        for h in range(HALVES):
            size = sb.tile([P, N], F32, name=f"size{h}")
            nc.scalar.activation(size[:], prod[h][:], ACT.Abs)
            shifted = sb.tile([P, N], F32, name=f"shifted{h}")
            denom = sb.tile([P, 1], F32, name=f"denom{h}")
            nc.vector.tensor_scalar(shifted[:], size[:], 0.2, None, ALU.add, ALU.max, accum_out=denom[:])
            inv = sb.tile([P, 1], F32, name=f"inv{h}")
            nc.vector.reciprocal(inv[:], denom[:])
            y = sb.tile([P, N], F32, name=f"y{h}")
            nc.vector.scalar_tensor_tensor(y[:], prod[h][:], inv[:], resid[h][:], ALU.mult, ALU.add)
            nc.sync.dma_start(out=out[half_cols(h), :], in_=y[:])
